import numpy as np
import ml_dtypes


def mxq(x, axis, fmt="e4m3"):
    dtype, down = {"e4m3": (ml_dtypes.float8_e4m3fn, 7), "e5m2": (ml_dtypes.float8_e5m2, 14)}[fmt]
    v = np.moveaxis(np.asarray(x, np.float32).astype(ml_dtypes.bfloat16).astype(np.float64), axis, -1)
    blocks = v.reshape(v.shape[:-1] + (-1, 32))
    amax = np.abs(blocks).max(-1, keepdims=True)
    byte = np.maximum(np.where(amax > 0, np.frexp(amax)[1] - 1 + 127, 0) - down, 1)
    scale = np.exp2(byte - 127.0)
    codes = (blocks / scale).astype(np.float32).astype(dtype).astype(np.float64)
    return np.moveaxis((codes * scale).reshape(v.shape), -1, axis)


WIDE = False


def mx_kscale(k):
    if not WIDE:
        return np.ones(k)
    levels = np.array([10, -10, 5, -5, 0])
    if k % 512:
        return np.exp2(np.random.permutation(np.resize(levels, k // 32))).repeat(32)
    a = np.empty((k // 512, 16))
    for p in range(k // 512):
        a[p, :8] = np.random.permutation(np.resize(levels, 8))
        for g in range(8):
            far = levels[np.abs(levels - a[p, g]) >= 10]
            a[p, g + 8] = far[np.random.randint(len(far))]
    return np.exp2(a.ravel()).repeat(32)


def f64(x):
    return np.asarray(x).astype(np.float64)


def striped(idx):
    return np.tile(np.asarray(idx).reshape(-1, 16).T, (8, 1)).astype(np.uint16)


def unstriped(offs):
    return offs[:16].T.reshape(-1).astype(np.int64)


E2M1 = np.array([0.0, 0.5, 1.0, 1.5, 2.0, 3.0, 4.0, 6.0, -0.0, -0.5, -1.0, -1.5, -2.0, -3.0, -4.0, -6.0])


def pack_weight(w, fmt):
    k, n = w.shape
    w = f64(np.asarray(w, np.float32).astype(ml_dtypes.bfloat16)).reshape(k // 32, 32, n)
    amax = np.abs(w).max(1)
    if fmt == "e4m3":
        byte = np.frexp(amax)[1] - 1 + 127 - 7
    else:
        mant, ex = np.frexp(amax / 6.0)
        byte = np.where(mant > 0.5, ex, ex - 1) + 127
    byte = np.clip(np.where(amax > 0, byte, 1), 1, 254)
    scaled = (w * np.exp2(127.0 - byte)[:, None, :]).reshape(k, n).astype(np.float32)
    by_word = np.ascontiguousarray(scaled.reshape(k // 512, 128, 4, n).transpose(0, 1, 3, 2))
    if fmt == "e4m3":
        words = by_word.astype(ml_dtypes.float8_e4m3fn).view(np.uint8)
    else:
        c = by_word.astype(ml_dtypes.float4_e2m1fn).view(np.uint8) & 0xF
        words = (c[..., 0::2] | (c[..., 1::2] << 4)).reshape(k // 512, 128, 2 * n)
    return np.ascontiguousarray(words), np.ascontiguousarray(byte.astype(np.uint8).reshape(k // 512, 16, n))


def unpack_weight(words, scales, fmt):
    g, _, n = scales.shape
    words = np.ascontiguousarray(words).reshape(g, 128, n, -1)
    if fmt == "e4m3":
        vals = words.view(ml_dtypes.float8_e4m3fn).astype(np.float64)
    else:
        nib = np.empty((g, 128, n, 4), np.uint8)
        nib[..., 0::2] = words & 0xF
        nib[..., 1::2] = words >> 4
        vals = E2M1[nib]
    vals = vals * np.repeat(np.exp2(scales.astype(np.float64) - 127.0), 8, axis=1)[..., None]
    return vals.transpose(0, 1, 3, 2).reshape(g * 512, n)


def bf(x):
    return np.asarray(x, np.float32).astype(ml_dtypes.bfloat16)


def planes(Y):
    r, m = Y.shape
    b = f64(bf(Y)).reshape(r // 32, 32, m)
    amax = np.abs(b).max(1)
    byte = np.clip(np.where(amax > 0, np.frexp(amax)[1] - 1 + 127 - 7, 1), 1, 254)
    codes = (b * np.exp2(127.0 - byte)[:, None, :]).reshape(r, m).astype(np.float32).astype(ml_dtypes.float8_e4m3fn).view(np.uint8)
    words = codes.reshape(r // 512, 128, 4, m).transpose(0, 1, 3, 2)
    return np.ascontiguousarray(words), np.ascontiguousarray(byte.astype(np.uint8).reshape(r // 512, 16, m))


D, T, I, Q, E, U, X = 512, 2048, 512, 256, 512, 1024, 1024


def setup_inputs():
    n = np.random.standard_normal
    idx = np.random.permutation(T)[:I]
    idx2 = np.random.permutation(U)[:Q]
    idx3 = np.random.permutation(U)[:Q]
    idx4 = np.random.permutation(X)[:I]
    fd = mx_kscale(D)
    fi = mx_kscale(I)
    keysp = pack_weight(n((D, T)) / fd[:, None], "e2m1")
    return {
        "users": (n((D, U)) * 1.0 / np.sqrt(D) * fd[:, None]).astype(np.float32),
        "keys_words": keysp[0],
        "keys_scales": keysp[1],
        "os": (np.random.uniform(0.02, 0.08, (1, I)) * fi).astype(np.float32),
        "vals": (n((E, T))).astype(np.float32),
        "vals2": (n((E, X))).astype(np.float32),
        "vsc": (np.random.uniform(0.5, 2.0, (1, I)) / fi).astype(np.float32),
        "offs": striped(idx),
        "offs2": striped(idx2),
        "offs3": striped(idx3),
        "offs4": striped(idx4),
    }


def reference(users, keys_words, keys_scales, os, vals, vals2, vsc, offs, offs2, offs3, offs4):
    idx = unstriped(offs)
    idx2 = unstriped(offs2)
    idx3 = unstriped(offs3)
    idx4 = unstriped(offs4)
    keysu = unpack_weight(keys_words, keys_scales, "e2m1")
    zq = np.maximum(f64(users)[:, idx2], f64(users)[:, idx3])
    zqq = mxq(zq, 0, "e4m3")
    keysidxg = keysu[:, idx]
    w = zqq.T @ keysidxg
    wo1 = w * f64(os)
    wt1 = wo1.T
    vz = np.maximum(f64(vals)[:, idx], f64(vals2)[:, idx4]) * f64(vsc)
    vt1 = vz.T
    vt1q = mxq(vt1, 0, "e4m3")
    wt1q = mxq(wt1, 0, "e4m3")
    o = vt1q.T @ wt1q
    words, scales = planes(o)
    return o, words, scales

@@ -1,0 +1,229 @@
+from contextlib import ExitStack
+
+import concourse.mybir as mybir
+from concourse.masks import make_identity
+
+D, T, I, Q, E, U, X = 512, 2048, 512, 256, 512, 1024, 1024
+FLOPS = 2 * Q * D * I + 2 * E * I * Q
+
+F32 = mybir.dt.float32
+BF16 = mybir.dt.bfloat16
+I32 = mybir.dt.int32
+U32 = mybir.dt.uint32
+U16 = mybir.dt.uint16
+U8 = mybir.dt.uint8
+FP8X4 = mybir.dt.float8_e4m3fn_x4
+FP4X4 = mybir.dt.float4_e2m1fn_x4
+COPY = mybir.ActivationFunctionType.Copy
+MAX = mybir.AluOpType.max
+MULT = mybir.AluOpType.mult
+
+P = 128
+PACK = 4
+RUN = 8
+BLOCKS = I // (PACK * RUN)
+HALF = Q // 2
+
+
+def tile_attend_querylarger_mergedvalues_lean_pl_kernel(
+    tc, users, keys_words, keys_scales, wsc, vals, vals2, vsc, offs, offs2, offs3, offs4, out_0, out_1, out_2
+):
+    nc = tc.nc
+    with ExitStack() as ctx:
+        lists = ctx.enter_context(tc.tile_pool(name="lists", bufs=1))
+        keep = ctx.enter_context(tc.tile_pool(name="keep", bufs=1))
+        work = ctx.enter_context(tc.tile_pool(name="work", bufs=4))
+        psum = ctx.enter_context(tc.psum_pool(name="psum", bufs=1))
+        turn = ctx.enter_context(tc.psum_pool(name="turn", bufs=2))
+
+        idx = lists.tile([P, I // 16], U16, name="idx")
+        idx2 = lists.tile([P, Q // 16], U16, name="idx2")
+        idx3 = lists.tile([P, Q // 16], U16, name="idx3")
+        idx4 = lists.tile([P, I // 16], U16, name="idx4")
+
+        users_p = users.rearrange("(p t) u -> t p u", t=PACK)
+        vals_p = vals.rearrange("(p j) c -> j p c", j=PACK)
+        vals2_p = vals2.rearrange("(p j) c -> j p c", j=PACK)
+        out_p = out_0.rearrange("(p j) q -> j p q", j=PACK)
+
+        user_pool = [keep.tile([P, U], F32, name=f"users{t}") for t in range(PACK)]
+        val_pool = [keep.tile([P, T], F32, name=f"vals{j}", tag=f"vals{j}") for j in range(PACK)]
+        val2_pool = [keep.tile([P, X], F32, name=f"second{j}") for j in range(PACK)]
+        key_pool = keep.tile([P, T], U16, name="key_pool")
+        scale_pool = keep.tile([P, T], U8, name="scale_pool")
+        factor_rows = keep.tile([2, I], F32, name="factor_rows")
+        factor_dealt = keep.tile([P, I], F32, name="factor_dealt")
+        ident = keep.tile([P, P], F32, name="ident")
+
+        nc.gpsimd.memset(scale_pool[:].bitcast(I32), 0)
+        nc.vector.memset(factor_dealt[:], 0.0)
+        make_identity(nc, ident[:])
+
+        def load_scale_rows(r):
+            nc.sync.dma_start(out=scale_pool[r:P:32, :].bitcast(I32), in_=keys_scales[0, r:16:4, :].bitcast(I32))
+
+        nc.scalar.dma_start(out=factor_rows[0:1, :], in_=wsc)
+        nc.scalar.dma_start(out=factor_rows[1:2, :], in_=vsc)
+        nc.sync.dma_start(out=key_pool[:].bitcast(I32), in_=keys_words[0].bitcast(I32))
+        nc.sync.dma_start(idx[:], offs)
+        nc.sync.dma_start(out=user_pool[0][:], in_=users_p[0])
+        nc.sync.dma_start(idx2[:], offs2)
+        nc.sync.dma_start(idx3[:], offs3)
+        nc.sync.dma_start(out=user_pool[1][:], in_=users_p[1])
+        nc.sync.dma_start(out=user_pool[2][:], in_=users_p[2])
+        for r in range(4):
+            load_scale_rows(r)
+        nc.sync.dma_start(out=user_pool[3][:], in_=users_p[3])
+        nc.sync.dma_start(out=val2_pool[0][:], in_=vals2_p[0])
+        nc.sync.dma_start(idx4[:], offs4)
+        nc.sync.dma_start(out=val_pool[0][:], in_=vals_p[0])
+        for j in range(1, PACK):
+            nc.sync.dma_start(out=val2_pool[j][:], in_=vals2_p[j])
+            nc.sync.dma_start(out=val_pool[j][:], in_=vals_p[j])
+
+        key_listed = keep.tile([P, I], U16, name="key_listed")
+        scale_listed = keep.tile([P, I], U8, name="scale_listed")
+        key_dealt = keep.tile([P, I], U16, name="key_dealt", align_bytes=64)
+        scale_dealt = keep.tile([P, I], U8, name="scale_dealt", align_bytes=64)
+        nc.vector.tensor_copy(key_listed[:], key_pool[:].indirect(idx[:]))
+        nc.vector.tensor_copy(scale_listed[:], scale_pool[:].indirect(idx[:]))
+        nc.vector.tensor_copy(
+            out=key_dealt[:].rearrange("p (t b r) -> p t b r", t=PACK, r=RUN),
+            in_=key_listed[:].rearrange("p (b t r) -> p t b r", t=PACK, r=RUN),
+        )
+        nc.vector.tensor_copy(
+            out=scale_dealt[:].bitcast(I32).rearrange("p (t b r) -> p t b r", t=PACK, r=RUN // 4),
+            in_=scale_listed[:].bitcast(I32).rearrange("p (b t r) -> p t b r", t=PACK, r=RUN // 4),
+        )
+
+        nc.scalar.copy(
+            out=factor_dealt[0:2, :].rearrange("k (t b r) -> k t b r", t=PACK, r=RUN),
+            in_=factor_rows[:].rearrange("k (b t r) -> k t b r", t=PACK, r=RUN),
+        )
+        factor_bank = psum.tile([P, PACK, P], F32, name="factor_bank")
+        for t in range(PACK):
+            nc.tensor.transpose(factor_bank[:, t, :], factor_dealt[:, t * P : (t + 1) * P], ident[:])
+        factors = keep.tile([P, 2, PACK], F32, name="factors")
+        nc.scalar.copy(out=factors[:], in_=factor_bank[:, :, 0:2].rearrange("p t k -> p k t"))
+
+        zq_rows = keep.tile([P, PACK, Q], BF16, name="zq_rows")
+        for t in range(PACK):
+            first = work.tile([P, Q], F32, name="first")
+            second = work.tile([P, Q], F32, name="second")
+            if t == PACK - 1:
+                nc.vector.tensor_copy(first[:], user_pool[t][:].indirect(idx2[:]))
+            else:
+                nc.scalar.activation(first[:], user_pool[t][:].indirect(idx2[:]), COPY)
+            nc.scalar.activation(second[:], user_pool[t][:].indirect(idx3[:]), COPY)
+            nc.vector.tensor_tensor(zq_rows[:, t, :], first[:], second[:], MAX)
+        zq_words = keep.tile([P, Q, PACK], BF16, name="zq_words", align_bytes=64)
+        nc.vector.tensor_copy(out=zq_words[:], in_=zq_rows[:].rearrange("p t q -> p q t"))
+        zq_codes = keep.tile([P, Q], U32, name="zq_codes", align_bytes=64)
+        zq_scales = keep.tile([P, Q], U8, name="zq_scales", align_bytes=64)
+        nc.vector.quantize_mx(
+            out=zq_codes[:].bitcast(FP8X4), scales=zq_scales[:], in_=zq_words[:].rearrange("p q t -> p (q t)")
+        )
+
+        wt_words = keep.tile([P, Q, PACK], BF16, name="wt_words", align_bytes=64)
+        wt_codes = keep.tile([P, Q], U32, name="wt_codes", align_bytes=64)
+        wt_scales = keep.tile([P, Q], U8, name="wt_scales", align_bytes=64)
+        for h in range(2):
+            cols = slice(h * HALF, (h + 1) * HALF)
+            bank = psum.tile([P, PACK, HALF], F32, name=f"score{h}")
+            for t in range(PACK):
+                nc.tensor.matmul_mx(
+                    out=bank[:, t, :],
+                    lhsT=key_dealt[:, t * P : (t + 1) * P].bitcast(U8).bitcast(FP4X4),
+                    lhsT_scale=scale_dealt[:, t * P : (t + 1) * P],
+                    rhs=zq_codes[:, cols].bitcast(FP8X4),
+                    rhs_scale=zq_scales[:, cols],
+                    start=True,
+                    stop=True,
+                )
+            nc.vector.tensor_tensor(
+                wt_words[:, cols, :],
+                bank[:].rearrange("p t q -> p q t"),
+                factors[:, 0, :].unsqueeze(1).to_broadcast([P, HALF, PACK]),
+                MULT,
+            )
+        nc.vector.quantize_mx(
+            out=wt_codes[:].bitcast(FP8X4), scales=wt_scales[:], in_=wt_words[:].rearrange("p q t -> p (q t)")
+        )
+
+        result = [psum.tile([P, PACK, HALF], F32, name=f"result{h}") for h in range(2)]
+        half_cols = I // 32
+
+        def store_rows(j, o_rows, queue):
+            for h in (1, 0):
+                nc.scalar.copy(out=o_rows[:, h * HALF : (h + 1) * HALF], in_=result[h][:, j, :])
+            queue.dma_start(out=out_p[j], in_=o_rows[:])
+
+        def multiply(j, turned, vt_words):
+            nc.vector.tensor_tensor(
+                vt_words[:],
+                turned[:].rearrange("p t m -> p m t"),
+                factors[:, 1, :].unsqueeze(1).to_broadcast([P, P, PACK]),
+                MULT,
+            )
+            vt_codes = work.tile([P, P], U32, name="vt_codes", align_bytes=64)
+            vt_scales = work.tile([P, P], U8, name="vt_scales", align_bytes=64)
+            nc.vector.quantize_mx(
+                out=vt_codes[:].bitcast(FP8X4), scales=vt_scales[:], in_=vt_words[:].rearrange("p m t -> p (m t)")
+            )
+            for h in range(2):
+                cols = slice(h * HALF, (h + 1) * HALF)
+                nc.tensor.matmul_mx(
+                    out=result[h][:, j, :],
+                    lhsT=vt_codes[:].bitcast(FP8X4),
+                    lhsT_scale=vt_scales[:],
+                    rhs=wt_codes[:, cols].bitcast(FP8X4),
+                    rhs_scale=wt_scales[:, cols],
+                    start=True,
+                    stop=True,
+                )
+
+        turned = []
+        for j in range(PACK):
+            first = work.tile([P, I], F32, name="vfirst")
+            second = keep.tile([P, I], F32, name=f"vsecond{j}", tag=f"vsecond{j}", align_bytes=64)
+            nc.scalar.activation(second[:], val2_pool[j][:].indirect(idx4[:]), COPY)
+            nc.vector.tensor_copy(first[:, : I // 2], val_pool[j][:].indirect(idx[:, :half_cols]))
+            nc.scalar.activation(first[:, I // 2 :], val_pool[j][:].indirect(idx[:, half_cols:]), COPY)
+            if j > 1:
+                store_rows(j - 2, keep.tile([P, Q], F32, name=f"o_rows{j - 2}", tag=f"vals{j}"), nc.sync)
+            larger = work.tile([P, I], F32, name="larger")
+            nc.vector.tensor_tensor(
+                larger[:].rearrange("p (t b r) -> p t b r", t=PACK, r=RUN),
+                first[:].rearrange("p (b t r) -> p t b r", t=PACK, r=RUN),
+                second[:].rearrange("p (b t r) -> p t b r", t=PACK, r=RUN),
+                MAX,
+            )
+            turned.append(turn.tile([P, PACK, P], F32, name="turned"))
+            for t in range(PACK):
+                nc.tensor.transpose(turned[j][:, t, :], larger[:, t * P : (t + 1) * P], ident[:])
+            if j > 0:
+                words = keep.tile([P, P, PACK], BF16, name=f"vt_words{j - 1}", tag=f"vsecond{j}", align_bytes=64)
+                multiply(j - 1, turned[j - 1], words)
+        store_rows(PACK - 2, keep.tile([P, Q], F32, name="o_rows_third"), nc.sync)
+        multiply(PACK - 1, turned[PACK - 1], keep.tile([P, P, PACK], BF16, name="vt_words_last", align_bytes=64))
+
+        o_words = [keep.tile([P, HALF, PACK], BF16, name=f"o_words{h}", align_bytes=64) for h in range(2)]
+        nc.vector.tensor_copy(out=o_words[0][:], in_=result[0][:].rearrange("p j q -> p q j"))
+        nc.scalar.copy(out=o_words[1][:], in_=result[1][:].rearrange("p j q -> p q j"))
+        store_rows(PACK - 1, keep.tile([P, Q], F32, name="o_rows_last"), nc.scalar)
+
+        o_codes = keep.tile([P, Q], U32, name="o_codes", align_bytes=64)
+        o_scales = keep.tile([P, Q], U8, name="o_scales", align_bytes=64)
+        for h in range(2):
+            cols = slice(h * HALF, (h + 1) * HALF)
+            nc.vector.quantize_mx(
+                out=o_codes[:, cols].bitcast(FP8X4),
+                scales=o_scales[:, cols],
+                in_=o_words[h][:].rearrange("p q j -> p (q j)"),
+            )
+        nc.sync.dma_start(out=out_1[0].rearrange("p c r -> p (c r)").bitcast(I32), in_=o_codes[:].bitcast(I32))
+        for g in range(4):
+            (nc.sync if g < 2 else nc.scalar).dma_start(
+                out=out_2[0, 4 * g : 4 * g + 4, :].bitcast(I32),
+                in_=o_scales[32 * g : 32 * g + 4, :].bitcast(I32),
+            )

@@ -23,6 +23,7 @@ PACK = 4
 RUN = 8
 BLOCKS = I // (PACK * RUN)
 HALF = Q // 2
+SHARE = 160
 
 
 def tile_attend_querylarger_mergedvalues_lean_pl_kernel(
@@ -44,7 +45,7 @@ def tile_attend_querylarger_mergedvalues_lean_pl_kernel(
         users_p = users.rearrange("(p t) u -> t p u", t=PACK)
         vals_p = vals.rearrange("(p j) c -> j p c", j=PACK)
         vals2_p = vals2.rearrange("(p j) c -> j p c", j=PACK)
-        out_p = out_0.rearrange("(p j) q -> j p q", j=PACK)
+        out_p = out_0.rearrange("(p j) q -> p j q", j=PACK)
 
         user_pool = [keep.tile([P, U], F32, name=f"users{t}") for t in range(PACK)]
         val_pool = [keep.tile([P, T], F32, name=f"vals{j}", tag=f"vals{j}") for j in range(PACK)]
@@ -59,21 +60,27 @@ def tile_attend_querylarger_mergedvalues_lean_pl_kernel(
         nc.vector.memset(factor_dealt[:], 0.0)
         make_identity(nc, ident[:])
 
+        def quantize(codes, scales, words):
+            nc.vector.quantize_mx(
+                out=codes[:].bitcast(FP8X4), scales=scales[:], in_=words[:].rearrange("p c t -> p (c t)")
+            )
+
         def load_scale_rows(r):
             nc.sync.dma_start(out=scale_pool[r:P:32, :].bitcast(I32), in_=keys_scales[0, r:16:4, :].bitcast(I32))
 
-        nc.scalar.dma_start(out=factor_rows[0:1, :], in_=wsc)
-        nc.scalar.dma_start(out=factor_rows[1:2, :], in_=vsc)
-        nc.sync.dma_start(out=key_pool[:].bitcast(I32), in_=keys_words[0].bitcast(I32))
-        nc.sync.dma_start(idx[:], offs)
         nc.sync.dma_start(out=user_pool[0][:], in_=users_p[0])
         nc.sync.dma_start(idx2[:], offs2)
         nc.sync.dma_start(idx3[:], offs3)
+        nc.sync.dma_start(out=key_pool[:].bitcast(I32), in_=keys_words[0].bitcast(I32))
+        nc.sync.dma_start(idx[:], offs)
         nc.sync.dma_start(out=user_pool[1][:], in_=users_p[1])
+        load_scale_rows(0)
         nc.sync.dma_start(out=user_pool[2][:], in_=users_p[2])
-        for r in range(4):
+        for r in range(1, 4):
             load_scale_rows(r)
         nc.sync.dma_start(out=user_pool[3][:], in_=users_p[3])
+        nc.sync.dma_start(out=factor_rows[0:1, :], in_=wsc)
+        nc.sync.dma_start(out=factor_rows[1:2, :], in_=vsc)
         nc.sync.dma_start(out=val2_pool[0][:], in_=vals2_p[0])
         nc.sync.dma_start(idx4[:], offs4)
         nc.sync.dma_start(out=val_pool[0][:], in_=vals_p[0])
@@ -96,7 +103,7 @@ def tile_attend_querylarger_mergedvalues_lean_pl_kernel(
             in_=scale_listed[:].bitcast(I32).rearrange("p (b t r) -> p t b r", t=PACK, r=RUN // 4),
         )
 
-        nc.scalar.copy(
+        nc.gpsimd.tensor_copy(
             out=factor_dealt[0:2, :].rearrange("k (t b r) -> k t b r", t=PACK, r=RUN),
             in_=factor_rows[:].rearrange("k (b t r) -> k t b r", t=PACK, r=RUN),
         )
@@ -104,59 +111,58 @@ def tile_attend_querylarger_mergedvalues_lean_pl_kernel(
         for t in range(PACK):
             nc.tensor.transpose(factor_bank[:, t, :], factor_dealt[:, t * P : (t + 1) * P], ident[:])
         factors = keep.tile([P, 2, PACK], F32, name="factors")
-        nc.scalar.copy(out=factors[:], in_=factor_bank[:, :, 0:2].rearrange("p t k -> p k t"))
+        nc.vector.tensor_copy(out=factors[:], in_=factor_bank[:, :, 0:2].rearrange("p t k -> p k t"))
 
         zq_rows = keep.tile([P, PACK, Q], BF16, name="zq_rows")
         for t in range(PACK):
             first = work.tile([P, Q], F32, name="first")
             second = work.tile([P, Q], F32, name="second")
-            if t == PACK - 1:
+            if t in (0, PACK - 1):
                 nc.vector.tensor_copy(first[:], user_pool[t][:].indirect(idx2[:]))
             else:
                 nc.scalar.activation(first[:], user_pool[t][:].indirect(idx2[:]), COPY)
             nc.scalar.activation(second[:], user_pool[t][:].indirect(idx3[:]), COPY)
             nc.vector.tensor_tensor(zq_rows[:, t, :], first[:], second[:], MAX)
-        zq_words = keep.tile([P, Q, PACK], BF16, name="zq_words", align_bytes=64)
-        nc.vector.tensor_copy(out=zq_words[:], in_=zq_rows[:].rearrange("p t q -> p q t"))
-        zq_codes = keep.tile([P, Q], U32, name="zq_codes", align_bytes=64)
-        zq_scales = keep.tile([P, Q], U8, name="zq_scales", align_bytes=64)
-        nc.vector.quantize_mx(
-            out=zq_codes[:].bitcast(FP8X4), scales=zq_scales[:], in_=zq_words[:].rearrange("p q t -> p (q t)")
-        )
-
-        wt_words = keep.tile([P, Q, PACK], BF16, name="wt_words", align_bytes=64)
-        wt_codes = keep.tile([P, Q], U32, name="wt_codes", align_bytes=64)
-        wt_scales = keep.tile([P, Q], U8, name="wt_scales", align_bytes=64)
+        zq_words = [keep.tile([P, HALF, PACK], BF16, name=f"zq_words{h}", align_bytes=64) for h in range(2)]
+        zq_codes = [keep.tile([P, HALF], U32, name=f"zq_codes{h}", align_bytes=64) for h in range(2)]
+        zq_scales = [keep.tile([P, HALF], U8, name=f"zq_scales{h}", align_bytes=64) for h in range(2)]
         for h in range(2):
-            cols = slice(h * HALF, (h + 1) * HALF)
+            nc.vector.tensor_copy(
+                out=zq_words[h][:], in_=zq_rows[:, :, h * HALF : (h + 1) * HALF].rearrange("p t q -> p q t")
+            )
+        for h in range(2):
+            quantize(zq_codes[h], zq_scales[h], zq_words[h])
+
+        wt_words = [keep.tile([P, HALF, PACK], BF16, name=f"wt_words{h}", align_bytes=64) for h in range(2)]
+        wt_codes = [keep.tile([P, HALF], U32, name=f"wt_codes{h}", align_bytes=64) for h in range(2)]
+        wt_scales = [keep.tile([P, HALF], U8, name=f"wt_scales{h}", align_bytes=64) for h in range(2)]
+        for h in range(2):
             bank = psum.tile([P, PACK, HALF], F32, name=f"score{h}")
             for t in range(PACK):
                 nc.tensor.matmul_mx(
                     out=bank[:, t, :],
                     lhsT=key_dealt[:, t * P : (t + 1) * P].bitcast(U8).bitcast(FP4X4),
                     lhsT_scale=scale_dealt[:, t * P : (t + 1) * P],
-                    rhs=zq_codes[:, cols].bitcast(FP8X4),
-                    rhs_scale=zq_scales[:, cols],
+                    rhs=zq_codes[h][:].bitcast(FP8X4),
+                    rhs_scale=zq_scales[h][:],
                     start=True,
                     stop=True,
                 )
             nc.vector.tensor_tensor(
-                wt_words[:, cols, :],
+                wt_words[h][:],
                 bank[:].rearrange("p t q -> p q t"),
                 factors[:, 0, :].unsqueeze(1).to_broadcast([P, HALF, PACK]),
                 MULT,
             )
-        nc.vector.quantize_mx(
-            out=wt_codes[:].bitcast(FP8X4), scales=wt_scales[:], in_=wt_words[:].rearrange("p q t -> p (q t)")
-        )
+        for h in range(2):
+            quantize(wt_codes[h], wt_scales[h], wt_words[h])
 
         result = [psum.tile([P, PACK, HALF], F32, name=f"result{h}") for h in range(2)]
-        half_cols = I // 32
 
-        def store_rows(j, o_rows, queue):
+        def store_rows(planes, o_rows, queue):
             for h in (1, 0):
-                nc.scalar.copy(out=o_rows[:, h * HALF : (h + 1) * HALF], in_=result[h][:, j, :])
-            queue.dma_start(out=out_p[j], in_=o_rows[:])
+                nc.scalar.copy(out=o_rows[:, :, h * HALF : (h + 1) * HALF], in_=result[h][:, planes, :])
+            queue.dma_start(out=out_p[:, planes, :], in_=o_rows[:])
 
         def multiply(j, turned, vt_words):
             nc.vector.tensor_tensor(
@@ -167,50 +173,50 @@ def tile_attend_querylarger_mergedvalues_lean_pl_kernel(
             )
             vt_codes = work.tile([P, P], U32, name="vt_codes", align_bytes=64)
             vt_scales = work.tile([P, P], U8, name="vt_scales", align_bytes=64)
-            nc.vector.quantize_mx(
-                out=vt_codes[:].bitcast(FP8X4), scales=vt_scales[:], in_=vt_words[:].rearrange("p m t -> p (m t)")
-            )
+            quantize(vt_codes, vt_scales, vt_words)
             for h in range(2):
-                cols = slice(h * HALF, (h + 1) * HALF)
                 nc.tensor.matmul_mx(
                     out=result[h][:, j, :],
                     lhsT=vt_codes[:].bitcast(FP8X4),
                     lhsT_scale=vt_scales[:],
-                    rhs=wt_codes[:, cols].bitcast(FP8X4),
-                    rhs_scale=wt_scales[:, cols],
+                    rhs=wt_codes[h][:].bitcast(FP8X4),
+                    rhs_scale=wt_scales[h][:],
                     start=True,
                     stop=True,
                 )
 
         turned = []
         for j in range(PACK):
-            first = work.tile([P, I], F32, name="vfirst")
-            second = keep.tile([P, I], F32, name=f"vsecond{j}", tag=f"vsecond{j}", align_bytes=64)
+            head = keep.tile([P, SHARE], F32, name=f"vhead{j}", tag=f"vhead{j}", align_bytes=64)
+            rest = work.tile([P, I - SHARE], F32, name="vrest")
+            second = work.tile([P, I], F32, name="vsecond")
             nc.scalar.activation(second[:], val2_pool[j][:].indirect(idx4[:]), COPY)
-            nc.vector.tensor_copy(first[:, : I // 2], val_pool[j][:].indirect(idx[:, :half_cols]))
-            nc.scalar.activation(first[:, I // 2 :], val_pool[j][:].indirect(idx[:, half_cols:]), COPY)
-            if j > 1:
-                store_rows(j - 2, keep.tile([P, Q], F32, name=f"o_rows{j - 2}", tag=f"vals{j}"), nc.sync)
+            nc.vector.tensor_copy(head[:], val_pool[j][:].indirect(idx[:, : SHARE // 16]))
+            nc.scalar.activation(rest[:], val_pool[j][:].indirect(idx[:, SHARE // 16 :]), COPY)
+            if j == PACK - 1:
+                store_rows(slice(0, 2), keep.tile([P, 2, Q], F32, name="o_rows_early", tag=f"vals{j}"), nc.sync)
             larger = work.tile([P, I], F32, name="larger")
-            nc.vector.tensor_tensor(
-                larger[:].rearrange("p (t b r) -> p t b r", t=PACK, r=RUN),
-                first[:].rearrange("p (b t r) -> p t b r", t=PACK, r=RUN),
-                second[:].rearrange("p (b t r) -> p t b r", t=PACK, r=RUN),
-                MAX,
-            )
+            dealt = larger[:].rearrange("p (t b r) -> p t b r", t=PACK, r=RUN)
+            for part, slots in ((head, slice(0, SHARE)), (rest, slice(SHARE, I))):
+                nc.vector.tensor_tensor(
+                    dealt[:, :, slots.start // 32 : slots.stop // 32, :],
+                    part[:].rearrange("p (b t r) -> p t b r", t=PACK, r=RUN),
+                    second[:, slots].rearrange("p (b t r) -> p t b r", t=PACK, r=RUN),
+                    MAX,
+                )
             turned.append(turn.tile([P, PACK, P], F32, name="turned"))
             for t in range(PACK):
                 nc.tensor.transpose(turned[j][:, t, :], larger[:, t * P : (t + 1) * P], ident[:])
             if j > 0:
-                words = keep.tile([P, P, PACK], BF16, name=f"vt_words{j - 1}", tag=f"vsecond{j}", align_bytes=64)
+                words = keep.tile([P, P, PACK], BF16, name=f"vt_words{j - 1}", tag=f"vhead{j}", align_bytes=64)
                 multiply(j - 1, turned[j - 1], words)
-        store_rows(PACK - 2, keep.tile([P, Q], F32, name="o_rows_third"), nc.sync)
+        store_rows(slice(2, 3), keep.tile([P, 1, Q], F32, name="o_rows_third"), nc.sync)
         multiply(PACK - 1, turned[PACK - 1], keep.tile([P, P, PACK], BF16, name="vt_words_last", align_bytes=64))
 
         o_words = [keep.tile([P, HALF, PACK], BF16, name=f"o_words{h}", align_bytes=64) for h in range(2)]
         nc.vector.tensor_copy(out=o_words[0][:], in_=result[0][:].rearrange("p j q -> p q j"))
         nc.scalar.copy(out=o_words[1][:], in_=result[1][:].rearrange("p j q -> p q j"))
-        store_rows(PACK - 1, keep.tile([P, Q], F32, name="o_rows_last"), nc.scalar)
+        store_rows(slice(3, 4), keep.tile([P, 1, Q], F32, name="o_rows_last"), nc.scalar)
 
         o_codes = keep.tile([P, Q], U32, name="o_codes", align_bytes=64)
         o_scales = keep.tile([P, Q], U8, name="o_scales", align_bytes=64)

@@ -62,7 +62,7 @@ def tile_attend_querylarger_mergedvalues_lean_pl_kernel(
 
         def quantize(codes, scales, words):
             nc.vector.quantize_mx(
-                out=codes[:].bitcast(FP8X4), scales=scales[:], in_=words[:].rearrange("p c t -> p (c t)")
+                out=codes.bitcast(FP8X4), scales=scales, in_=words.rearrange("p c t -> p (c t)")
             )
 
         def load_scale_rows(r):
@@ -103,7 +103,7 @@ def tile_attend_querylarger_mergedvalues_lean_pl_kernel(
             in_=scale_listed[:].bitcast(I32).rearrange("p (b t r) -> p t b r", t=PACK, r=RUN // 4),
         )
 
-        nc.gpsimd.tensor_copy(
+        nc.scalar.copy(
             out=factor_dealt[0:2, :].rearrange("k (t b r) -> k t b r", t=PACK, r=RUN),
             in_=factor_rows[:].rearrange("k (b t r) -> k t b r", t=PACK, r=RUN),
         )
@@ -131,7 +131,7 @@ def tile_attend_querylarger_mergedvalues_lean_pl_kernel(
                 out=zq_words[h][:], in_=zq_rows[:, :, h * HALF : (h + 1) * HALF].rearrange("p t q -> p q t")
             )
         for h in range(2):
-            quantize(zq_codes[h], zq_scales[h], zq_words[h])
+            quantize(zq_codes[h][:], zq_scales[h][:], zq_words[h][:])
 
         wt_words = [keep.tile([P, HALF, PACK], BF16, name=f"wt_words{h}", align_bytes=64) for h in range(2)]
         wt_codes = [keep.tile([P, HALF], U32, name=f"wt_codes{h}", align_bytes=64) for h in range(2)]
@@ -155,7 +155,7 @@ def tile_attend_querylarger_mergedvalues_lean_pl_kernel(
                 MULT,
             )
         for h in range(2):
-            quantize(wt_codes[h], wt_scales[h], wt_words[h])
+            quantize(wt_codes[h][:], wt_scales[h][:], wt_words[h][:])
 
         result = [psum.tile([P, PACK, HALF], F32, name=f"result{h}") for h in range(2)]
 
@@ -164,17 +164,20 @@ def tile_attend_querylarger_mergedvalues_lean_pl_kernel(
                 nc.scalar.copy(out=o_rows[:, :, h * HALF : (h + 1) * HALF], in_=result[h][:, planes, :])
             queue.dma_start(out=out_p[:, planes, :], in_=o_rows[:])
 
-        def multiply(j, turned, vt_words):
-            nc.vector.tensor_tensor(
-                vt_words[:],
-                turned[:].rearrange("p t m -> p m t"),
-                factors[:, 1, :].unsqueeze(1).to_broadcast([P, P, PACK]),
-                MULT,
-            )
+        def multiply(j, turned, vt_words, pieces):
             vt_codes = work.tile([P, P], U32, name="vt_codes", align_bytes=64)
             vt_scales = work.tile([P, P], U8, name="vt_scales", align_bytes=64)
-            quantize(vt_codes, vt_scales, vt_words)
-            for h in range(2):
+            cuts = [slice(c * P // pieces, (c + 1) * P // pieces) for c in range(pieces)]
+            for cols in cuts:
+                nc.vector.tensor_tensor(
+                    vt_words[:, cols, :],
+                    turned[:, :, cols].rearrange("p t m -> p m t"),
+                    factors[:, 1, :].unsqueeze(1).to_broadcast([P, P // pieces, PACK]),
+                    MULT,
+                )
+            for cols in cuts:
+                quantize(vt_codes[:, cols], vt_scales[:, cols], vt_words[:, cols, :])
+            for h in (1, 0):
                 nc.tensor.matmul_mx(
                     out=result[h][:, j, :],
                     lhsT=vt_codes[:].bitcast(FP8X4),
@@ -197,11 +200,15 @@ def tile_attend_querylarger_mergedvalues_lean_pl_kernel(
                 store_rows(slice(0, 2), keep.tile([P, 2, Q], F32, name="o_rows_early", tag=f"vals{j}"), nc.sync)
             larger = work.tile([P, I], F32, name="larger")
             dealt = larger[:].rearrange("p (t b r) -> p t b r", t=PACK, r=RUN)
-            for part, slots in ((head, slice(0, SHARE)), (rest, slice(SHARE, I))):
+            for part, slots, places in (
+                (head, slice(0, SHARE), slice(0, PACK)),
+                (rest, slice(SHARE, I), slice(0, 2)),
+                (rest, slice(SHARE, I), slice(2, PACK)),
+            ):
                 nc.vector.tensor_tensor(
-                    dealt[:, :, slots.start // 32 : slots.stop // 32, :],
-                    part[:].rearrange("p (b t r) -> p t b r", t=PACK, r=RUN),
-                    second[:, slots].rearrange("p (b t r) -> p t b r", t=PACK, r=RUN),
+                    dealt[:, places, slots.start // 32 : slots.stop // 32, :],
+                    part[:].rearrange("p (b t r) -> p t b r", t=PACK, r=RUN)[:, places],
+                    second[:, slots].rearrange("p (b t r) -> p t b r", t=PACK, r=RUN)[:, places],
                     MAX,
                 )
             turned.append(turn.tile([P, PACK, P], F32, name="turned"))
@@ -209,9 +216,9 @@ def tile_attend_querylarger_mergedvalues_lean_pl_kernel(
                 nc.tensor.transpose(turned[j][:, t, :], larger[:, t * P : (t + 1) * P], ident[:])
             if j > 0:
                 words = keep.tile([P, P, PACK], BF16, name=f"vt_words{j - 1}", tag=f"vhead{j}", align_bytes=64)
-                multiply(j - 1, turned[j - 1], words)
+                multiply(j - 1, turned[j - 1], words, 1)
         store_rows(slice(2, 3), keep.tile([P, 1, Q], F32, name="o_rows_third"), nc.sync)
-        multiply(PACK - 1, turned[PACK - 1], keep.tile([P, P, PACK], BF16, name="vt_words_last", align_bytes=64))
+        multiply(PACK - 1, turned[PACK - 1], keep.tile([P, P, PACK], BF16, name="vt_words_last", align_bytes=64), 2)
 
         o_words = [keep.tile([P, HALF, PACK], BF16, name=f"o_words{h}", align_bytes=64) for h in range(2)]
         nc.vector.tensor_copy(out=o_words[0][:], in_=result[0][:].rearrange("p j q -> p q j"))
@@ -220,13 +227,9 @@ def tile_attend_querylarger_mergedvalues_lean_pl_kernel(
 
         o_codes = keep.tile([P, Q], U32, name="o_codes", align_bytes=64)
         o_scales = keep.tile([P, Q], U8, name="o_scales", align_bytes=64)
-        for h in range(2):
+        for h in (1, 0):
             cols = slice(h * HALF, (h + 1) * HALF)
-            nc.vector.quantize_mx(
-                out=o_codes[:, cols].bitcast(FP8X4),
-                scales=o_scales[:, cols],
-                in_=o_words[h][:].rearrange("p q j -> p (q j)"),
-            )
+            quantize(o_codes[:, cols], o_scales[:, cols], o_words[h][:])
         nc.sync.dma_start(out=out_1[0].rearrange("p c r -> p (c r)").bitcast(I32), in_=o_codes[:].bitcast(I32))
         for g in range(4):
             (nc.sync if g < 2 else nc.scalar).dma_start(

@@ -59,6 +59,8 @@ def tile_attend_querylarger_mergedvalues_lean_pl_kernel(
         nc.gpsimd.memset(scale_pool[:].bitcast(I32), 0)
         nc.vector.memset(factor_dealt[:], 0.0)
         make_identity(nc, ident[:])
+        warm = keep.tile([P, 1], F32, name="warm")
+        nc.scalar.activation(warm[:], factor_dealt[:, 0:1], COPY)
 
         def quantize(codes, scales, words):
             nc.vector.quantize_mx(

from contextlib import ExitStack

import concourse.mybir as mybir
from concourse.masks import make_identity

D, T, I, Q, E, U, X = 512, 2048, 512, 256, 512, 1024, 1024
FLOPS = 2 * Q * D * I + 2 * E * I * Q

F32 = mybir.dt.float32
BF16 = mybir.dt.bfloat16
I32 = mybir.dt.int32
U32 = mybir.dt.uint32
U16 = mybir.dt.uint16
U8 = mybir.dt.uint8
FP8X4 = mybir.dt.float8_e4m3fn_x4
FP4X4 = mybir.dt.float4_e2m1fn_x4
COPY = mybir.ActivationFunctionType.Copy
MAX = mybir.AluOpType.max
MULT = mybir.AluOpType.mult

P = 128
PACK = 4
RUN = 8
BLOCKS = I // (PACK * RUN)
HALF = Q // 2
SHARE = 160


def tile_attend_querylarger_mergedvalues_lean_pl_kernel(
    tc, users, keys_words, keys_scales, wsc, vals, vals2, vsc, offs, offs2, offs3, offs4, out_0, out_1, out_2
):
    nc = tc.nc
    with ExitStack() as ctx:
        lists = ctx.enter_context(tc.tile_pool(name="lists", bufs=1))
        keep = ctx.enter_context(tc.tile_pool(name="keep", bufs=1))
        work = ctx.enter_context(tc.tile_pool(name="work", bufs=4))
        psum = ctx.enter_context(tc.psum_pool(name="psum", bufs=1))
        turn = ctx.enter_context(tc.psum_pool(name="turn", bufs=2))

        idx = lists.tile([P, I // 16], U16, name="idx")
        idx2 = lists.tile([P, Q // 16], U16, name="idx2")
        idx3 = lists.tile([P, Q // 16], U16, name="idx3")
        idx4 = lists.tile([P, I // 16], U16, name="idx4")

        users_p = users.rearrange("(p t) u -> t p u", t=PACK)
        vals_p = vals.rearrange("(p j) c -> j p c", j=PACK)
        vals2_p = vals2.rearrange("(p j) c -> j p c", j=PACK)
        out_p = out_0.rearrange("(p j) q -> p j q", j=PACK)

        user_pool = [keep.tile([P, U], F32, name=f"users{t}") for t in range(PACK)]
        val_pool = [keep.tile([P, T], F32, name=f"vals{j}", tag=f"vals{j}") for j in range(PACK)]
        val2_pool = [keep.tile([P, X], F32, name=f"second{j}") for j in range(PACK)]
        key_pool = keep.tile([P, T], U16, name="key_pool")
        scale_pool = keep.tile([P, T], U8, name="scale_pool")
        factor_rows = keep.tile([2, I], F32, name="factor_rows")
        factor_dealt = keep.tile([P, I], F32, name="factor_dealt")
        ident = keep.tile([P, P], F32, name="ident")

        nc.gpsimd.memset(scale_pool[:].bitcast(I32), 0)
        nc.vector.memset(factor_dealt[:], 0.0)
        make_identity(nc, ident[:])
        warm = keep.tile([P, 1], F32, name="warm")
        nc.scalar.activation(warm[:], factor_dealt[:, 0:1], COPY)

        def quantize(codes, scales, words):
            nc.vector.quantize_mx(
                out=codes.bitcast(FP8X4), scales=scales, in_=words.rearrange("p c t -> p (c t)")
            )

        def load_scale_rows(r):
            nc.sync.dma_start(out=scale_pool[r:P:32, :].bitcast(I32), in_=keys_scales[0, r:16:4, :].bitcast(I32))

        nc.sync.dma_start(out=user_pool[0][:], in_=users_p[0])
        nc.sync.dma_start(idx2[:], offs2)
        nc.sync.dma_start(idx3[:], offs3)
        nc.sync.dma_start(out=key_pool[:].bitcast(I32), in_=keys_words[0].bitcast(I32))
        nc.sync.dma_start(idx[:], offs)
        nc.sync.dma_start(out=user_pool[1][:], in_=users_p[1])
        load_scale_rows(0)
        nc.sync.dma_start(out=user_pool[2][:], in_=users_p[2])
        for r in range(1, 4):
            load_scale_rows(r)
        nc.sync.dma_start(out=user_pool[3][:], in_=users_p[3])
        nc.sync.dma_start(out=factor_rows[0:1, :], in_=wsc)
        nc.sync.dma_start(out=factor_rows[1:2, :], in_=vsc)
        nc.sync.dma_start(out=val2_pool[0][:], in_=vals2_p[0])
        nc.sync.dma_start(idx4[:], offs4)
        nc.sync.dma_start(out=val_pool[0][:], in_=vals_p[0])
        for j in range(1, PACK):
            nc.sync.dma_start(out=val2_pool[j][:], in_=vals2_p[j])
            nc.sync.dma_start(out=val_pool[j][:], in_=vals_p[j])

        key_listed = keep.tile([P, I], U16, name="key_listed")
        scale_listed = keep.tile([P, I], U8, name="scale_listed")
        key_dealt = keep.tile([P, I], U16, name="key_dealt", align_bytes=64)
        scale_dealt = keep.tile([P, I], U8, name="scale_dealt", align_bytes=64)
        nc.vector.tensor_copy(key_listed[:], key_pool[:].indirect(idx[:]))
        nc.vector.tensor_copy(scale_listed[:], scale_pool[:].indirect(idx[:]))
        nc.vector.tensor_copy(
            out=key_dealt[:].rearrange("p (t b r) -> p t b r", t=PACK, r=RUN),
            in_=key_listed[:].rearrange("p (b t r) -> p t b r", t=PACK, r=RUN),
        )
        nc.vector.tensor_copy(
            out=scale_dealt[:].bitcast(I32).rearrange("p (t b r) -> p t b r", t=PACK, r=RUN // 4),
            in_=scale_listed[:].bitcast(I32).rearrange("p (b t r) -> p t b r", t=PACK, r=RUN // 4),
        )

        nc.scalar.copy(
            out=factor_dealt[0:2, :].rearrange("k (t b r) -> k t b r", t=PACK, r=RUN),
            in_=factor_rows[:].rearrange("k (b t r) -> k t b r", t=PACK, r=RUN),
        )
        factor_bank = psum.tile([P, PACK, P], F32, name="factor_bank")
        for t in range(PACK):
            nc.tensor.transpose(factor_bank[:, t, :], factor_dealt[:, t * P : (t + 1) * P], ident[:])
        factors = keep.tile([P, 2, PACK], F32, name="factors")
        nc.vector.tensor_copy(out=factors[:], in_=factor_bank[:, :, 0:2].rearrange("p t k -> p k t"))

        zq_rows = keep.tile([P, PACK, Q], BF16, name="zq_rows")
        for t in range(PACK):
            first = work.tile([P, Q], F32, name="first")
            second = work.tile([P, Q], F32, name="second")
            if t in (0, PACK - 1):
                nc.vector.tensor_copy(first[:], user_pool[t][:].indirect(idx2[:]))
            else:
                nc.scalar.activation(first[:], user_pool[t][:].indirect(idx2[:]), COPY)
            nc.scalar.activation(second[:], user_pool[t][:].indirect(idx3[:]), COPY)
            nc.vector.tensor_tensor(zq_rows[:, t, :], first[:], second[:], MAX)
        zq_words = [keep.tile([P, HALF, PACK], BF16, name=f"zq_words{h}", align_bytes=64) for h in range(2)]
        zq_codes = [keep.tile([P, HALF], U32, name=f"zq_codes{h}", align_bytes=64) for h in range(2)]
        zq_scales = [keep.tile([P, HALF], U8, name=f"zq_scales{h}", align_bytes=64) for h in range(2)]
        for h in range(2):
            nc.vector.tensor_copy(
                out=zq_words[h][:], in_=zq_rows[:, :, h * HALF : (h + 1) * HALF].rearrange("p t q -> p q t")
            )
        for h in range(2):
            quantize(zq_codes[h][:], zq_scales[h][:], zq_words[h][:])

        wt_words = [keep.tile([P, HALF, PACK], BF16, name=f"wt_words{h}", align_bytes=64) for h in range(2)]
        wt_codes = [keep.tile([P, HALF], U32, name=f"wt_codes{h}", align_bytes=64) for h in range(2)]
        wt_scales = [keep.tile([P, HALF], U8, name=f"wt_scales{h}", align_bytes=64) for h in range(2)]
        for h in range(2):
            bank = psum.tile([P, PACK, HALF], F32, name=f"score{h}")
            for t in range(PACK):
                nc.tensor.matmul_mx(
                    out=bank[:, t, :],
                    lhsT=key_dealt[:, t * P : (t + 1) * P].bitcast(U8).bitcast(FP4X4),
                    lhsT_scale=scale_dealt[:, t * P : (t + 1) * P],
                    rhs=zq_codes[h][:].bitcast(FP8X4),
                    rhs_scale=zq_scales[h][:],
                    start=True,
                    stop=True,
                )
            nc.vector.tensor_tensor(
                wt_words[h][:],
                bank[:].rearrange("p t q -> p q t"),
                factors[:, 0, :].unsqueeze(1).to_broadcast([P, HALF, PACK]),
                MULT,
            )
        for h in range(2):
            quantize(wt_codes[h][:], wt_scales[h][:], wt_words[h][:])

        result = [psum.tile([P, PACK, HALF], F32, name=f"result{h}") for h in range(2)]

        def store_rows(planes, o_rows, queue):
            for h in (1, 0):
                nc.scalar.copy(out=o_rows[:, :, h * HALF : (h + 1) * HALF], in_=result[h][:, planes, :])
            queue.dma_start(out=out_p[:, planes, :], in_=o_rows[:])

        def multiply(j, turned, vt_words, pieces):
            vt_codes = work.tile([P, P], U32, name="vt_codes", align_bytes=64)
            vt_scales = work.tile([P, P], U8, name="vt_scales", align_bytes=64)
            cuts = [slice(c * P // pieces, (c + 1) * P // pieces) for c in range(pieces)]
            for cols in cuts:
                nc.vector.tensor_tensor(
                    vt_words[:, cols, :],
                    turned[:, :, cols].rearrange("p t m -> p m t"),
                    factors[:, 1, :].unsqueeze(1).to_broadcast([P, P // pieces, PACK]),
                    MULT,
                )
            for cols in cuts:
                quantize(vt_codes[:, cols], vt_scales[:, cols], vt_words[:, cols, :])
            for h in (1, 0):
                nc.tensor.matmul_mx(
                    out=result[h][:, j, :],
                    lhsT=vt_codes[:].bitcast(FP8X4),
                    lhsT_scale=vt_scales[:],
                    rhs=wt_codes[h][:].bitcast(FP8X4),
                    rhs_scale=wt_scales[h][:],
                    start=True,
                    stop=True,
                )

        turned = []
        for j in range(PACK):
            head = keep.tile([P, SHARE], F32, name=f"vhead{j}", tag=f"vhead{j}", align_bytes=64)
            rest = work.tile([P, I - SHARE], F32, name="vrest")
            second = work.tile([P, I], F32, name="vsecond")
            nc.scalar.activation(second[:], val2_pool[j][:].indirect(idx4[:]), COPY)
            nc.vector.tensor_copy(head[:], val_pool[j][:].indirect(idx[:, : SHARE // 16]))
            nc.scalar.activation(rest[:], val_pool[j][:].indirect(idx[:, SHARE // 16 :]), COPY)
            if j == PACK - 1:
                store_rows(slice(0, 2), keep.tile([P, 2, Q], F32, name="o_rows_early", tag=f"vals{j}"), nc.sync)
            larger = work.tile([P, I], F32, name="larger")
            dealt = larger[:].rearrange("p (t b r) -> p t b r", t=PACK, r=RUN)
            for part, slots, places in (
                (head, slice(0, SHARE), slice(0, PACK)),
                (rest, slice(SHARE, I), slice(0, 2)),
                (rest, slice(SHARE, I), slice(2, PACK)),
            ):
                nc.vector.tensor_tensor(
                    dealt[:, places, slots.start // 32 : slots.stop // 32, :],
                    part[:].rearrange("p (b t r) -> p t b r", t=PACK, r=RUN)[:, places],
                    second[:, slots].rearrange("p (b t r) -> p t b r", t=PACK, r=RUN)[:, places],
                    MAX,
                )
            turned.append(turn.tile([P, PACK, P], F32, name="turned"))
            for t in range(PACK):
                nc.tensor.transpose(turned[j][:, t, :], larger[:, t * P : (t + 1) * P], ident[:])
            if j > 0:
                words = keep.tile([P, P, PACK], BF16, name=f"vt_words{j - 1}", tag=f"vhead{j}", align_bytes=64)
                multiply(j - 1, turned[j - 1], words, 1)
        store_rows(slice(2, 3), keep.tile([P, 1, Q], F32, name="o_rows_third"), nc.sync)
        multiply(PACK - 1, turned[PACK - 1], keep.tile([P, P, PACK], BF16, name="vt_words_last", align_bytes=64), 2)

        o_words = [keep.tile([P, HALF, PACK], BF16, name=f"o_words{h}", align_bytes=64) for h in range(2)]
        nc.vector.tensor_copy(out=o_words[0][:], in_=result[0][:].rearrange("p j q -> p q j"))
        nc.scalar.copy(out=o_words[1][:], in_=result[1][:].rearrange("p j q -> p q j"))
        store_rows(slice(3, 4), keep.tile([P, 1, Q], F32, name="o_rows_last"), nc.scalar)

        o_codes = keep.tile([P, Q], U32, name="o_codes", align_bytes=64)
        o_scales = keep.tile([P, Q], U8, name="o_scales", align_bytes=64)
        for h in (1, 0):
            cols = slice(h * HALF, (h + 1) * HALF)
            quantize(o_codes[:, cols], o_scales[:, cols], o_words[h][:])
        nc.sync.dma_start(out=out_1[0].rearrange("p c r -> p (c r)").bitcast(I32), in_=o_codes[:].bitcast(I32))
        for g in range(4):
            (nc.sync if g < 2 else nc.scalar).dma_start(
                out=out_2[0, 4 * g : 4 * g + 4, :].bitcast(I32),
                in_=o_scales[32 * g : 32 * g + 4, :].bitcast(I32),
            )
